import numpy as np
import ml_dtypes


def mxq(x, axis, fmt="e4m3"):
    dtype, down = {"e4m3": (ml_dtypes.float8_e4m3fn, 7), "e5m2": (ml_dtypes.float8_e5m2, 14)}[fmt]
    v = np.moveaxis(np.asarray(x, np.float32).astype(ml_dtypes.bfloat16).astype(np.float64), axis, -1)
    blocks = v.reshape(v.shape[:-1] + (-1, 32))
    amax = np.abs(blocks).max(-1, keepdims=True)
    byte = np.maximum(np.where(amax > 0, np.frexp(amax)[1] - 1 + 127, 0) - down, 1)
    scale = np.exp2(byte - 127.0)
    codes = (blocks / scale).astype(np.float32).astype(dtype).astype(np.float64)
    return np.moveaxis((codes * scale).reshape(v.shape), -1, axis)


WIDE = False


def mx_kscale(k):
    if not WIDE:
        return np.ones(k)
    levels = np.array([10, -10, 5, -5, 0])
    if k % 512:
        return np.exp2(np.random.permutation(np.resize(levels, k // 32))).repeat(32)
    a = np.empty((k // 512, 16))
    for p in range(k // 512):
        a[p, :8] = np.random.permutation(np.resize(levels, 8))
        for g in range(8):
            far = levels[np.abs(levels - a[p, g]) >= 10]
            a[p, g + 8] = far[np.random.randint(len(far))]
    return np.exp2(a.ravel()).repeat(32)


def f64(x):
    return np.asarray(x).astype(np.float64)


def striped(idx):
    return np.tile(idx.reshape(-1, 16).T, (8, 1)).astype(np.uint16)


def unstriped(offs):
    return offs[:16].T.reshape(-1).astype(np.int64)


def silu(v):
    return v / (1.0 + np.exp(-np.maximum(v, -700.0)))


K, T, D, S, V, H, N = 1536, 1024, 4, 512, 256, 512, 512


def setup_inputs():
    n = np.random.standard_normal
    s = mx_kscale(K)[:, None]
    u = mx_kscale(H)
    return {
        "xT": (n((K, T)) * s).astype(np.float32),
        "w1": (n((K, H)) / np.sqrt(K) / s * u).astype(np.float32),
        "w2": (n((H, N)) / np.sqrt(H) / u[:, None]).astype(np.float32),
        "gate": np.tile(np.random.uniform(0.2, 1.0, (D, 1, V)) / np.sqrt(D), (1, N, 1)).astype(np.float32),
        "offs": striped(np.random.permutation(T)[:S]),
        "pos1": striped(np.random.permutation(S)[:V]),
        "pos2": striped(np.random.permutation(S)[:V]),
        "pos3": striped(np.random.permutation(S)[:V]),
        "pos4": striped(np.random.permutation(S)[:V]),
    }


def reference(xT, w1, w2, gate, offs, pos1, pos2, pos3, pos4):
    idx = unstriped(offs)
    xq = mxq(f64(xT)[:, idx], 0, "e4m3")
    h = silu(mxq(f64(w1), 0, "e4m3").T @ xq)
    y = mxq(f64(w2), 0, "e4m3").T @ mxq(h, 0, "e4m3")
    return sum(f64(gate[d]) * y[:, unstriped(p)] for d, p in enumerate((pos1, pos2, pos3, pos4)))

@@ -1,0 +1,240 @@
+from contextlib import ExitStack
+
+import concourse.mybir as mybir
+
+K, T, S, H, N, V, D = 1536, 1024, 512, 512, 512, 256, 4
+FLOPS = 2 * K * H * S + 2 * H * N * S
+
+F32 = mybir.dt.float32
+BF16 = mybir.dt.bfloat16
+U32 = mybir.dt.uint32
+U16 = mybir.dt.uint16
+U8 = mybir.dt.uint8
+FP8X4 = mybir.dt.float8_e4m3fn_x4
+COPY = mybir.ActivationFunctionType.Copy
+SILU = mybir.ActivationFunctionType.Silu
+MULT = mybir.AluOpType.mult
+ADD = mybir.AluOpType.add
+
+P = 128
+G = K // 512
+M_TILES = N // P
+PIECE = 256
+A = 256
+
+
+def tile_picked_sub_mlp_silu_sub_e_kernel(tc, xT, w1, w2, gate, offs, pos1, pos2, pos3, pos4, out):
+    nc = tc.nc
+    with ExitStack() as ctx:
+        keep = ctx.enter_context(tc.tile_pool(name="keep", bufs=1))
+        psum = ctx.enter_context(tc.psum_pool(name="psum", bufs=1))
+
+        def sb(name, shape, dtype):
+            return keep.tile(shape, dtype, name=name, align_bytes=64)
+
+        offs_sb = sb("offs_sb", [P, S // 16], U16)
+        pos_sb = [sb(f"pos_sb{d}", [P, V // 16], U16) for d in range(D)]
+        x_raw = [sb(f"x_raw{g}", [P, 4, T], F32) for g in range(G)]
+        x_grp = [[sb(f"x_grp{g}_{i}", [P, PIECE, 4], BF16) for i in range(T // PIECE)] for g in range(G)]
+        x_words = [sb(f"x_words{g}", [P, T], U32) for g in range(G)]
+        x_bytes = sb("x_bytes", [P, T], U8)
+        p_words = [sb(f"p_words{g}", [P, S], U32) for g in range(G)]
+        p_bytes = sb("p_bytes", [P, S], U8)
+        w1_raw = [sb(f"w1_raw{g}", [P, 4, H], F32) for g in range(G)]
+        w1_grp = [sb(f"w1_grp{g}", [P, 4 * H], BF16) for g in range(G)]
+        w1_words = [sb(f"w1_words{g}", [P, H], U32) for g in range(G)]
+        w1_bytes = [sb(f"w1_bytes{g}", [P, H], U8) for g in range(G)]
+        w2_raw = sb("w2_raw", [P, 4, N], F32)
+        w2_grp = [sb(f"w2_grp{m}", [P, P, 4], BF16) for m in range(M_TILES)]
+        w2_words = [sb(f"w2_words{m}", [P, P], U32) for m in range(M_TILES)]
+        w2_bytes = [sb(f"w2_bytes{m}", [P, P], U8) for m in range(M_TILES)]
+        h_flat = sb("h_flat", [P, 4, A], BF16)
+        h_grp_a = sb("h_grp_a", [P, A, 4], BF16)
+        h_grp_b = [sb(f"h_grp_b{s}", [P, P, 4], BF16) for s in range(2)]
+        h_words = sb("h_words", [P, S], U32)
+        h_bytes = sb("h_bytes", [P, S], U8)
+        gates = [sb(f"gates{m}", [P, D, V], F32) for m in range(M_TILES)]
+        y_sb = [sb(f"y_sb{m}", [P, S], F32) for m in range(M_TILES)]
+        terms = [sb(f"terms{m}", [P, D, V], F32) for m in range(M_TILES)]
+        pairs = [sb(f"pairs{m}", [P, 2, V], F32) for m in range(M_TILES)]
+        sums = [sb(f"sums{m}", [P, V], F32) for m in range(M_TILES)]
+        warm = sb("warm", [P, 1], F32)
+
+        def load_x(g):
+            nc.sync.dma_start(out=x_raw[g][:], in_=xT[512 * g : 512 * (g + 1), :].rearrange("(p j) t -> p j t", j=4))
+
+        load_x(0)
+        nc.sync.dma_start(offs_sb[:], offs)
+        load_x(1)
+        load_x(2)
+        for g in range(G):
+            nc.sync.dma_start(out=w1_raw[g][:], in_=w1[512 * g : 512 * (g + 1), :].rearrange("(p j) c -> p j c", j=4))
+        nc.sync.dma_start(out=w2_raw[:], in_=w2.rearrange("(p j) c -> p j c", j=4))
+        for d, pos in enumerate((pos1, pos2, pos3, pos4)):
+            nc.sync.dma_start(pos_sb[d][:], pos)
+        for m in range(M_TILES):
+            nc.sync.dma_start(out=gates[m][:], in_=gate[:, P * m : P * (m + 1), :].rearrange("d p v -> p d v"))
+
+        nc.gpsimd.memset(x_bytes[:], 0)
+        nc.vector.memset(warm[:], 0.0)
+        nc.scalar.activation(warm[:], warm[:], SILU)
+
+        def cast_x(g, i):
+            src = x_raw[g][:, :, PIECE * i : PIECE * (i + 1)].rearrange("p j (c i) -> p c j i", i=4)
+            dst = x_grp[g][i][:].rearrange("p (c i) j -> p c j i", i=4)
+            if i == 0:
+                nc.vector.tensor_copy(dst, src)
+            else:
+                nc.scalar.activation(dst, src, COPY)
+
+        def quant_x(g, i):
+            cols = slice(PIECE * i, PIECE * (i + 1))
+            nc.vector.quantize_mx(
+                out=x_words[g][:, cols].bitcast(FP8X4),
+                scales=x_bytes[4 * g : P, cols],
+                in_=x_grp[g][i][:].rearrange("p c j -> p (c j)"),
+            )
+
+        def cast_w1(g, engine, m0, m1):
+            src = w1_raw[g][:].rearrange("p j (m t) -> p m t j", t=4)[:, m0:m1]
+            dst = w1_grp[g][:].rearrange("p (t m j) -> p m t j", t=4, j=4)[:, m0:m1]
+            if engine == "v":
+                nc.vector.tensor_copy(dst, src)
+            else:
+                nc.scalar.activation(dst, src, COPY)
+
+        def quant_w1(g, t0, t1):
+            nc.vector.quantize_mx(
+                out=w1_words[g][:, P * t0 : P * t1].bitcast(FP8X4),
+                scales=w1_bytes[g][:, P * t0 : P * t1],
+                in_=w1_grp[g][:, 512 * t0 : 512 * t1],
+            )
+
+        for g in range(G):
+            for i in range(T // PIECE):
+                cast_x(g, i)
+            for i in range(T // PIECE):
+                quant_x(g, i)
+            nc.vector.tensor_copy(p_words[g][:], x_words[g][:].indirect(offs_sb[:]))
+        nc.vector.tensor_copy(p_bytes[:], x_bytes[:].indirect(offs_sb[:]))
+
+        acc_a = [psum.tile([P, A], F32, name=f"acc_a{t}") for t in range(4)]
+        acc_b = [psum.tile([P, 4, P], F32, name=f"acc_b{s}") for s in range(2)]
+
+        def layer1(dst, t, c0, c1, g):
+            nc.tensor.matmul_mx(
+                out=dst,
+                lhsT=w1_words[g][:, P * t : P * (t + 1)].bitcast(FP8X4),
+                lhsT_scale=w1_bytes[g][:, P * t : P * (t + 1)],
+                rhs=p_words[g][:, c0:c1].bitcast(FP8X4),
+                rhs_scale=p_bytes[4 * g : P, c0:c1],
+                start=(g == 0),
+                stop=(g == G - 1),
+            )
+
+        def layer1_b(s, t, g):
+            layer1(acc_b[s][:, t, :], t, A + P * s, A + P * (s + 1), g)
+
+        for g in range(G):
+            split = 64 if g < 2 else 48
+            cast_w1(g, "s", 0, split)
+            cast_w1(g, "v", split, P)
+            if g < 2:
+                quant_w1(g, 0, 4)
+            else:
+                quant_w1(g, 0, 1)
+                quant_w1(g, 1, 2)
+                quant_w1(g, 2, 4)
+            for t in range(4):
+                layer1(acc_a[t][:], t, 0, A, g)
+            for s in range(2):
+                layer1_b(s, 0, g)
+        for s in range(2):
+            for t in range(1, 4):
+                for g in range(G):
+                    layer1_b(s, t, g)
+
+        def cast_w2(m):
+            src = w2_raw[:, :, P * m : P * (m + 1)].rearrange("p j (c i) -> p c j i", i=4)
+            dst = w2_grp[m][:].rearrange("p (c i) j -> p c j i", i=4)
+            if m == 0:
+                nc.vector.tensor_copy(dst, src)
+            else:
+                nc.scalar.activation(dst, src, COPY)
+
+        def quant_w2(m):
+            nc.vector.quantize_mx(
+                out=w2_words[m][:].bitcast(FP8X4),
+                scales=w2_bytes[m][:],
+                in_=w2_grp[m][:].rearrange("p c j -> p (c j)"),
+            )
+
+        for t in range(4):
+            nc.scalar.activation(h_flat[:, t, :], acc_a[t][:], SILU)
+        for s in range(2):
+            nc.scalar.activation(h_grp_b[s][:], acc_b[s][:].rearrange("p t n -> p n t"), SILU)
+
+        cast_w2(0)
+        nc.vector.tensor_copy(h_grp_a[:], h_flat[:].rearrange("p t n -> p n t"))
+        quant_w2(0)
+
+        def quant_h(grp, c0, c1):
+            nc.vector.quantize_mx(
+                out=h_words[:, c0:c1].bitcast(FP8X4),
+                scales=h_bytes[:, c0:c1],
+                in_=grp[:].rearrange("p n t -> p (n t)"),
+            )
+
+        quant_h(h_grp_a, 0, A)
+        for s in range(2):
+            quant_h(h_grp_b[s], A + P * s, A + P * (s + 1))
+
+        tags = ("acc_y0", "acc_y1", "acc_a0", "acc_a1")
+        acc_y = [psum.tile([P, S], F32, name=f"acc_y{m}", tag=tags[m]) for m in range(M_TILES)]
+
+        def layer2(m):
+            for c0, c1 in ((0, A), (A, A + P), (A + P, S)):
+                nc.tensor.matmul_mx(
+                    out=acc_y[m][:, c0:c1],
+                    lhsT=w2_words[m][:].bitcast(FP8X4),
+                    lhsT_scale=w2_bytes[m][:],
+                    rhs=h_words[:, c0:c1].bitcast(FP8X4),
+                    rhs_scale=h_bytes[:, c0:c1],
+                    start=True,
+                    stop=True,
+                )
+
+        layer2(0)
+        for c0, c1 in ((0, A + P), (A + P, S)):
+            nc.vector.tensor_copy(y_sb[0][:, c0:c1], acc_y[0][:, c0:c1])
+        for m in range(1, M_TILES):
+            cast_w2(m)
+            quant_w2(m)
+            layer2(m)
+            nc.scalar.activation(y_sb[m][:], acc_y[m][:], COPY)
+
+        def fetch(m, d):
+            nc.vector.tensor_tensor(terms[m][:, d, :], y_sb[m][:].indirect(pos_sb[d][:]), gates[m][:, d, :], MULT)
+
+        def add(o, a, b):
+            nc.vector.tensor_tensor(o, a, b, ADD)
+
+        def store(m):
+            nc.sync.dma_start(out=out[P * m : P * (m + 1), :], in_=sums[m][:])
+
+        for m in range(M_TILES):
+            fetch(m, 0)
+            if m > 0:
+                add(pairs[m - 1][:], terms[m - 1][:, 0:2, :], terms[m - 1][:, 2:4, :])
+            fetch(m, 1)
+            if m > 0:
+                add(sums[m - 1][:], pairs[m - 1][:, 0, :], pairs[m - 1][:, 1, :])
+                store(m - 1)
+            fetch(m, 2)
+            if m == M_TILES - 1:
+                add(pairs[m][:, 0, :], terms[m][:, 0, :], terms[m][:, 1, :])
+            fetch(m, 3)
+        m = M_TILES - 1
+        add(pairs[m][:, 1, :], pairs[m][:, 0, :], terms[m][:, 2, :])
+        add(sums[m][:], pairs[m][:, 1, :], terms[m][:, 3, :])
+        store(m)

@@ -19,7 +19,6 @@ ADD = mybir.AluOpType.add
 P = 128
 G = K // 512
 M_TILES = N // P
-PIECE = 256
 A = 256
 
 
@@ -34,8 +33,14 @@ def tile_picked_sub_mlp_silu_sub_e_kernel(tc, xT, w1, w2, gate, offs, pos1, pos2
 
         offs_sb = sb("offs_sb", [P, S // 16], U16)
         pos_sb = [sb(f"pos_sb{d}", [P, V // 16], U16) for d in range(D)]
-        x_raw = [sb(f"x_raw{g}", [P, 4, T], F32) for g in range(G)]
-        x_grp = [[sb(f"x_grp{g}_{i}", [P, PIECE, 4], BF16) for i in range(T // PIECE)] for g in range(G)]
+        loads = [[(0, T // 2), (T // 2, T)]] * G
+        pieces = [
+            [(0, 256, "s"), (256, 512, "s"), (512, 768, "v"), (768, 1024, "s")],
+            [(0, 256, "s"), (256, 512, "s"), (512, 768, "v"), (768, 1024, "s")],
+            [(0, 256, "s"), (256, 512, "v"), (512, 768, "s"), (768, 1024, "v")],
+        ]
+        x_raw = [[sb(f"x_raw{g}_{t0}", [P, 4, t1 - t0], F32) for t0, t1 in loads[g]] for g in range(G)]
+        x_grp = [[sb(f"x_grp{g}_{t0}", [P, t1 - t0, 4], BF16) for t0, t1, e in pieces[g]] for g in range(G)]
         x_words = [sb(f"x_words{g}", [P, T], U32) for g in range(G)]
         x_bytes = sb("x_bytes", [P, T], U8)
         p_words = [sb(f"p_words{g}", [P, S], U32) for g in range(G)]
@@ -45,9 +50,9 @@ def tile_picked_sub_mlp_silu_sub_e_kernel(tc, xT, w1, w2, gate, offs, pos1, pos2
         w1_words = [sb(f"w1_words{g}", [P, H], U32) for g in range(G)]
         w1_bytes = [sb(f"w1_bytes{g}", [P, H], U8) for g in range(G)]
         w2_raw = sb("w2_raw", [P, 4, N], F32)
-        w2_grp = [sb(f"w2_grp{m}", [P, P, 4], BF16) for m in range(M_TILES)]
-        w2_words = [sb(f"w2_words{m}", [P, P], U32) for m in range(M_TILES)]
-        w2_bytes = [sb(f"w2_bytes{m}", [P, P], U8) for m in range(M_TILES)]
+        w2_grp = sb("w2_grp", [P, N, 4], BF16)
+        w2_words = sb("w2_words", [P, N], U32)
+        w2_bytes = sb("w2_bytes", [P, N], U8)
         h_flat = sb("h_flat", [P, 4, A], BF16)
         h_grp_a = sb("h_grp_a", [P, A, 4], BF16)
         h_grp_b = [sb(f"h_grp_b{s}", [P, P, 4], BF16) for s in range(2)]
@@ -61,7 +66,9 @@ def tile_picked_sub_mlp_silu_sub_e_kernel(tc, xT, w1, w2, gate, offs, pos1, pos2
         warm = sb("warm", [P, 1], F32)
 
         def load_x(g):
-            nc.sync.dma_start(out=x_raw[g][:], in_=xT[512 * g : 512 * (g + 1), :].rearrange("(p j) t -> p j t", j=4))
+            rows = xT[512 * g : 512 * (g + 1), :].rearrange("(p j) t -> p j t", j=4)
+            for raw, (t0, t1) in zip(x_raw[g], loads[g]):
+                nc.sync.dma_start(out=raw[:], in_=rows[:, :, t0:t1])
 
         load_x(0)
         nc.sync.dma_start(offs_sb[:], offs)
@@ -80,18 +87,21 @@ def tile_picked_sub_mlp_silu_sub_e_kernel(tc, xT, w1, w2, gate, offs, pos1, pos2
         nc.scalar.activation(warm[:], warm[:], SILU)
 
         def cast_x(g, i):
-            src = x_raw[g][:, :, PIECE * i : PIECE * (i + 1)].rearrange("p j (c i) -> p c j i", i=4)
+            t0, t1, engine = pieces[g][i]
+            for raw, (l0, l1) in zip(x_raw[g], loads[g]):
+                if l0 <= t0 and t1 <= l1:
+                    src = raw[:, :, t0 - l0 : t1 - l0].rearrange("p j (c i) -> p c j i", i=4)
             dst = x_grp[g][i][:].rearrange("p (c i) j -> p c j i", i=4)
-            if i == 0:
+            if engine == "v":
                 nc.vector.tensor_copy(dst, src)
             else:
                 nc.scalar.activation(dst, src, COPY)
 
         def quant_x(g, i):
-            cols = slice(PIECE * i, PIECE * (i + 1))
+            t0, t1, engine = pieces[g][i]
             nc.vector.quantize_mx(
-                out=x_words[g][:, cols].bitcast(FP8X4),
-                scales=x_bytes[4 * g : P, cols],
+                out=x_words[g][:, t0:t1].bitcast(FP8X4),
+                scales=x_bytes[4 * g : P, t0:t1],
                 in_=x_grp[g][i][:].rearrange("p c j -> p (c j)"),
             )
 
@@ -111,10 +121,11 @@ def tile_picked_sub_mlp_silu_sub_e_kernel(tc, xT, w1, w2, gate, offs, pos1, pos2
             )
 
         for g in range(G):
-            for i in range(T // PIECE):
-                cast_x(g, i)
-            for i in range(T // PIECE):
-                quant_x(g, i)
+            for half in ((0, 1), (2, 3)):
+                for i in half:
+                    cast_x(g, i)
+                for i in half:
+                    quant_x(g, i)
             nc.vector.tensor_copy(p_words[g][:], x_words[g][:].indirect(offs_sb[:]))
         nc.vector.tensor_copy(p_bytes[:], x_bytes[:].indirect(offs_sb[:]))
 
@@ -136,9 +147,10 @@ def tile_picked_sub_mlp_silu_sub_e_kernel(tc, xT, w1, w2, gate, offs, pos1, pos2
             layer1(acc_b[s][:, t, :], t, A + P * s, A + P * (s + 1), g)
 
         for g in range(G):
-            split = 64 if g < 2 else 48
+            split = (P, 64, 40)[g]
             cast_w1(g, "s", 0, split)
-            cast_w1(g, "v", split, P)
+            if split < P:
+                cast_w1(g, "v", split, P)
             if g < 2:
                 quant_w1(g, 0, 4)
             else:
@@ -154,29 +166,19 @@ def tile_picked_sub_mlp_silu_sub_e_kernel(tc, xT, w1, w2, gate, offs, pos1, pos2
                 for g in range(G):
                     layer1_b(s, t, g)
 
-        def cast_w2(m):
-            src = w2_raw[:, :, P * m : P * (m + 1)].rearrange("p j (c i) -> p c j i", i=4)
-            dst = w2_grp[m][:].rearrange("p (c i) j -> p c j i", i=4)
-            if m == 0:
-                nc.vector.tensor_copy(dst, src)
-            else:
-                nc.scalar.activation(dst, src, COPY)
-
-        def quant_w2(m):
-            nc.vector.quantize_mx(
-                out=w2_words[m][:].bitcast(FP8X4),
-                scales=w2_bytes[m][:],
-                in_=w2_grp[m][:].rearrange("p c j -> p (c j)"),
-            )
+        nc.vector.tensor_copy(
+            w2_grp[:].rearrange("p (c i) j -> p c j i", i=4), w2_raw[:].rearrange("p j (c i) -> p c j i", i=4)
+        )
+        nc.vector.quantize_mx(
+            out=w2_words[:].bitcast(FP8X4), scales=w2_bytes[:], in_=w2_grp[:].rearrange("p c j -> p (c j)")
+        )
 
         for t in range(4):
             nc.scalar.activation(h_flat[:, t, :], acc_a[t][:], SILU)
         for s in range(2):
             nc.scalar.activation(h_grp_b[s][:], acc_b[s][:].rearrange("p t n -> p n t"), SILU)
 
-        cast_w2(0)
         nc.vector.tensor_copy(h_grp_a[:], h_flat[:].rearrange("p t n -> p n t"))
-        quant_w2(0)
 
         def quant_h(grp, c0, c1):
             nc.vector.quantize_mx(
@@ -196,8 +198,8 @@ def tile_picked_sub_mlp_silu_sub_e_kernel(tc, xT, w1, w2, gate, offs, pos1, pos2
             for c0, c1 in ((0, A), (A, A + P), (A + P, S)):
                 nc.tensor.matmul_mx(
                     out=acc_y[m][:, c0:c1],
-                    lhsT=w2_words[m][:].bitcast(FP8X4),
-                    lhsT_scale=w2_bytes[m][:],
+                    lhsT=w2_words[:, P * m : P * (m + 1)].bitcast(FP8X4),
+                    lhsT_scale=w2_bytes[:, P * m : P * (m + 1)],
                     rhs=h_words[:, c0:c1].bitcast(FP8X4),
                     rhs_scale=h_bytes[:, c0:c1],
                     start=True,
@@ -208,8 +210,6 @@ def tile_picked_sub_mlp_silu_sub_e_kernel(tc, xT, w1, w2, gate, offs, pos1, pos2
         for c0, c1 in ((0, A + P), (A + P, S)):
             nc.vector.tensor_copy(y_sb[0][:, c0:c1], acc_y[0][:, c0:c1])
         for m in range(1, M_TILES):
-            cast_w2(m)
-            quant_w2(m)
             layer2(m)
             nc.scalar.activation(y_sb[m][:], acc_y[m][:], COPY)
 

@@ -33,14 +33,9 @@ def tile_picked_sub_mlp_silu_sub_e_kernel(tc, xT, w1, w2, gate, offs, pos1, pos2
 
         offs_sb = sb("offs_sb", [P, S // 16], U16)
         pos_sb = [sb(f"pos_sb{d}", [P, V // 16], U16) for d in range(D)]
-        loads = [[(0, T // 2), (T // 2, T)]] * G
-        pieces = [
-            [(0, 256, "s"), (256, 512, "s"), (512, 768, "v"), (768, 1024, "s")],
-            [(0, 256, "s"), (256, 512, "s"), (512, 768, "v"), (768, 1024, "s")],
-            [(0, 256, "s"), (256, 512, "v"), (512, 768, "s"), (768, 1024, "v")],
-        ]
-        x_raw = [[sb(f"x_raw{g}_{t0}", [P, 4, t1 - t0], F32) for t0, t1 in loads[g]] for g in range(G)]
-        x_grp = [[sb(f"x_grp{g}_{t0}", [P, t1 - t0, 4], BF16) for t0, t1, e in pieces[g]] for g in range(G)]
+        pieces = [(0, 256, "s"), (512, 768, "v"), (256, 512, "s"), (768, 1024, "v")]
+        x_raw = [sb(f"x_raw{g}", [P, 4, T], F32) for g in range(G)]
+        x_grp = [[sb(f"x_grp{g}_{t0}", [P, t1 - t0, 4], BF16) for t0, t1, e in pieces] for g in range(G)]
         x_words = [sb(f"x_words{g}", [P, T], U32) for g in range(G)]
         x_bytes = sb("x_bytes", [P, T], U8)
         p_words = [sb(f"p_words{g}", [P, S], U32) for g in range(G)]
@@ -66,9 +61,7 @@ def tile_picked_sub_mlp_silu_sub_e_kernel(tc, xT, w1, w2, gate, offs, pos1, pos2
         warm = sb("warm", [P, 1], F32)
 
         def load_x(g):
-            rows = xT[512 * g : 512 * (g + 1), :].rearrange("(p j) t -> p j t", j=4)
-            for raw, (t0, t1) in zip(x_raw[g], loads[g]):
-                nc.sync.dma_start(out=raw[:], in_=rows[:, :, t0:t1])
+            nc.sync.dma_start(out=x_raw[g][:], in_=xT[512 * g : 512 * (g + 1), :].rearrange("(p j) t -> p j t", j=4))
 
         load_x(0)
         nc.sync.dma_start(offs_sb[:], offs)
@@ -80,17 +73,17 @@ def tile_picked_sub_mlp_silu_sub_e_kernel(tc, xT, w1, w2, gate, offs, pos1, pos2
         for d, pos in enumerate((pos1, pos2, pos3, pos4)):
             nc.sync.dma_start(pos_sb[d][:], pos)
         for m in range(M_TILES):
-            nc.sync.dma_start(out=gates[m][:], in_=gate[:, P * m : P * (m + 1), :].rearrange("d p v -> p d v"))
+            for d0, d1 in ((0, 2), (2, 4)) if m == 0 else ((0, 4),):
+                rows = gate[d0:d1, P * m : P * (m + 1), :].rearrange("d p v -> p d v")
+                nc.sync.dma_start(out=gates[m][:, d0:d1, :], in_=rows)
 
         nc.gpsimd.memset(x_bytes[:], 0)
         nc.vector.memset(warm[:], 0.0)
         nc.scalar.activation(warm[:], warm[:], SILU)
 
         def cast_x(g, i):
-            t0, t1, engine = pieces[g][i]
-            for raw, (l0, l1) in zip(x_raw[g], loads[g]):
-                if l0 <= t0 and t1 <= l1:
-                    src = raw[:, :, t0 - l0 : t1 - l0].rearrange("p j (c i) -> p c j i", i=4)
+            t0, t1, engine = pieces[i]
+            src = x_raw[g][:, :, t0:t1].rearrange("p j (c i) -> p c j i", i=4)
             dst = x_grp[g][i][:].rearrange("p (c i) j -> p c j i", i=4)
             if engine == "v":
                 nc.vector.tensor_copy(dst, src)
@@ -98,16 +91,16 @@ def tile_picked_sub_mlp_silu_sub_e_kernel(tc, xT, w1, w2, gate, offs, pos1, pos2
                 nc.scalar.activation(dst, src, COPY)
 
         def quant_x(g, i):
-            t0, t1, engine = pieces[g][i]
+            t0, t1, engine = pieces[i]
             nc.vector.quantize_mx(
                 out=x_words[g][:, t0:t1].bitcast(FP8X4),
                 scales=x_bytes[4 * g : P, t0:t1],
                 in_=x_grp[g][i][:].rearrange("p c j -> p (c j)"),
             )
 
-        def cast_w1(g, engine, m0, m1):
-            src = w1_raw[g][:].rearrange("p j (m t) -> p m t j", t=4)[:, m0:m1]
-            dst = w1_grp[g][:].rearrange("p (t m j) -> p m t j", t=4, j=4)[:, m0:m1]
+        def cast_w1(g, engine, m0, m1, ts=slice(0, 4)):
+            src = w1_raw[g][:].rearrange("p j (m t) -> p m j t", t=4)[:, m0:m1, :, ts]
+            dst = w1_grp[g][:].rearrange("p (t m j) -> p m j t", t=4, j=4)[:, m0:m1, :, ts]
             if engine == "v":
                 nc.vector.tensor_copy(dst, src)
             else:
@@ -147,10 +140,11 @@ def tile_picked_sub_mlp_silu_sub_e_kernel(tc, xT, w1, w2, gate, offs, pos1, pos2
             layer1(acc_b[s][:, t, :], t, A + P * s, A + P * (s + 1), g)
 
         for g in range(G):
-            split = (P, 64, 40)[g]
+            split = (P, 64, 44)[g]
             cast_w1(g, "s", 0, split)
             if split < P:
-                cast_w1(g, "v", split, P)
+                cast_w1(g, "v", split, P, slice(0, 2))
+                cast_w1(g, "v", split, P, slice(2, 4))
             if g < 2:
                 quant_w1(g, 0, 4)
             else:
@@ -178,7 +172,9 @@ def tile_picked_sub_mlp_silu_sub_e_kernel(tc, xT, w1, w2, gate, offs, pos1, pos2
         for s in range(2):
             nc.scalar.activation(h_grp_b[s][:], acc_b[s][:].rearrange("p t n -> p n t"), SILU)
 
-        nc.vector.tensor_copy(h_grp_a[:], h_flat[:].rearrange("p t n -> p n t"))
+        nc.vector.tensor_copy(
+            h_grp_a[:].rearrange("p (c i) t -> p c t i", i=4), h_flat[:].rearrange("p t (c i) -> p c t i", i=4)
+        )
 
         def quant_h(grp, c0, c1):
             nc.vector.quantize_mx(
@@ -207,8 +203,8 @@ def tile_picked_sub_mlp_silu_sub_e_kernel(tc, xT, w1, w2, gate, offs, pos1, pos2
                 )
 
         layer2(0)
-        for c0, c1 in ((0, A + P), (A + P, S)):
-            nc.vector.tensor_copy(y_sb[0][:, c0:c1], acc_y[0][:, c0:c1])
+        nc.vector.tensor_copy(y_sb[0][:, : A + P], acc_y[0][:, : A + P])
+        nc.scalar.activation(y_sb[0][:, A + P :], acc_y[0][:, A + P :], COPY)
         for m in range(1, M_TILES):
             layer2(m)
             nc.scalar.activation(y_sb[m][:], acc_y[m][:], COPY)

from contextlib import ExitStack

import concourse.mybir as mybir

K, T, S, H, N, V, D = 1536, 1024, 512, 512, 512, 256, 4
FLOPS = 2 * K * H * S + 2 * H * N * S

F32 = mybir.dt.float32
BF16 = mybir.dt.bfloat16
U32 = mybir.dt.uint32
U16 = mybir.dt.uint16
U8 = mybir.dt.uint8
FP8X4 = mybir.dt.float8_e4m3fn_x4
COPY = mybir.ActivationFunctionType.Copy
SILU = mybir.ActivationFunctionType.Silu
MULT = mybir.AluOpType.mult
ADD = mybir.AluOpType.add

P = 128
G = K // 512
M_TILES = N // P
A = 256


def tile_picked_sub_mlp_silu_sub_e_kernel(tc, xT, w1, w2, gate, offs, pos1, pos2, pos3, pos4, out):
    nc = tc.nc
    with ExitStack() as ctx:
        keep = ctx.enter_context(tc.tile_pool(name="keep", bufs=1))
        psum = ctx.enter_context(tc.psum_pool(name="psum", bufs=1))

        def sb(name, shape, dtype):
            return keep.tile(shape, dtype, name=name, align_bytes=64)

        offs_sb = sb("offs_sb", [P, S // 16], U16)
        pos_sb = [sb(f"pos_sb{d}", [P, V // 16], U16) for d in range(D)]
        pieces = [(0, 256, "s"), (512, 768, "v"), (256, 512, "s"), (768, 1024, "v")]
        x_raw = [sb(f"x_raw{g}", [P, 4, T], F32) for g in range(G)]
        x_grp = [[sb(f"x_grp{g}_{t0}", [P, t1 - t0, 4], BF16) for t0, t1, e in pieces] for g in range(G)]
        x_words = [sb(f"x_words{g}", [P, T], U32) for g in range(G)]
        x_bytes = sb("x_bytes", [P, T], U8)
        p_words = [sb(f"p_words{g}", [P, S], U32) for g in range(G)]
        p_bytes = sb("p_bytes", [P, S], U8)
        w1_raw = [sb(f"w1_raw{g}", [P, 4, H], F32) for g in range(G)]
        w1_grp = [sb(f"w1_grp{g}", [P, 4 * H], BF16) for g in range(G)]
        w1_words = [sb(f"w1_words{g}", [P, H], U32) for g in range(G)]
        w1_bytes = [sb(f"w1_bytes{g}", [P, H], U8) for g in range(G)]
        w2_raw = sb("w2_raw", [P, 4, N], F32)
        w2_grp = sb("w2_grp", [P, N, 4], BF16)
        w2_words = sb("w2_words", [P, N], U32)
        w2_bytes = sb("w2_bytes", [P, N], U8)
        h_flat = sb("h_flat", [P, 4, A], BF16)
        h_grp_a = sb("h_grp_a", [P, A, 4], BF16)
        h_grp_b = [sb(f"h_grp_b{s}", [P, P, 4], BF16) for s in range(2)]
        h_words = sb("h_words", [P, S], U32)
        h_bytes = sb("h_bytes", [P, S], U8)
        gates = [sb(f"gates{m}", [P, D, V], F32) for m in range(M_TILES)]
        y_sb = [sb(f"y_sb{m}", [P, S], F32) for m in range(M_TILES)]
        terms = [sb(f"terms{m}", [P, D, V], F32) for m in range(M_TILES)]
        pairs = [sb(f"pairs{m}", [P, 2, V], F32) for m in range(M_TILES)]
        sums = [sb(f"sums{m}", [P, V], F32) for m in range(M_TILES)]
        warm = sb("warm", [P, 1], F32)

        def load_x(g):
            nc.sync.dma_start(out=x_raw[g][:], in_=xT[512 * g : 512 * (g + 1), :].rearrange("(p j) t -> p j t", j=4))

        load_x(0)
        nc.sync.dma_start(offs_sb[:], offs)
        load_x(1)
        load_x(2)
        for g in range(G):
            nc.sync.dma_start(out=w1_raw[g][:], in_=w1[512 * g : 512 * (g + 1), :].rearrange("(p j) c -> p j c", j=4))
        nc.sync.dma_start(out=w2_raw[:], in_=w2.rearrange("(p j) c -> p j c", j=4))
        for d, pos in enumerate((pos1, pos2, pos3, pos4)):
            nc.sync.dma_start(pos_sb[d][:], pos)
        for m in range(M_TILES):
            for d0, d1 in ((0, 2), (2, 4)) if m == 0 else ((0, 4),):
                rows = gate[d0:d1, P * m : P * (m + 1), :].rearrange("d p v -> p d v")
                nc.sync.dma_start(out=gates[m][:, d0:d1, :], in_=rows)

        nc.gpsimd.memset(x_bytes[:], 0)
        nc.vector.memset(warm[:], 0.0)
        nc.scalar.activation(warm[:], warm[:], SILU)

        def cast_x(g, i):
            t0, t1, engine = pieces[i]
            src = x_raw[g][:, :, t0:t1].rearrange("p j (c i) -> p c j i", i=4)
            dst = x_grp[g][i][:].rearrange("p (c i) j -> p c j i", i=4)
            if engine == "v":
                nc.vector.tensor_copy(dst, src)
            else:
                nc.scalar.activation(dst, src, COPY)

        def quant_x(g, i):
            t0, t1, engine = pieces[i]
            nc.vector.quantize_mx(
                out=x_words[g][:, t0:t1].bitcast(FP8X4),
                scales=x_bytes[4 * g : P, t0:t1],
                in_=x_grp[g][i][:].rearrange("p c j -> p (c j)"),
            )

        def cast_w1(g, engine, m0, m1, ts=slice(0, 4)):
            src = w1_raw[g][:].rearrange("p j (m t) -> p m j t", t=4)[:, m0:m1, :, ts]
            dst = w1_grp[g][:].rearrange("p (t m j) -> p m j t", t=4, j=4)[:, m0:m1, :, ts]
            if engine == "v":
                nc.vector.tensor_copy(dst, src)
            else:
                nc.scalar.activation(dst, src, COPY)

        def quant_w1(g, t0, t1):
            nc.vector.quantize_mx(
                out=w1_words[g][:, P * t0 : P * t1].bitcast(FP8X4),
                scales=w1_bytes[g][:, P * t0 : P * t1],
                in_=w1_grp[g][:, 512 * t0 : 512 * t1],
            )

        for g in range(G):
            for half in ((0, 1), (2, 3)):
                for i in half:
                    cast_x(g, i)
                for i in half:
                    quant_x(g, i)
            nc.vector.tensor_copy(p_words[g][:], x_words[g][:].indirect(offs_sb[:]))
        nc.vector.tensor_copy(p_bytes[:], x_bytes[:].indirect(offs_sb[:]))

        acc_a = [psum.tile([P, A], F32, name=f"acc_a{t}") for t in range(4)]
        acc_b = [psum.tile([P, 4, P], F32, name=f"acc_b{s}") for s in range(2)]

        def layer1(dst, t, c0, c1, g):
            nc.tensor.matmul_mx(
                out=dst,
                lhsT=w1_words[g][:, P * t : P * (t + 1)].bitcast(FP8X4),
                lhsT_scale=w1_bytes[g][:, P * t : P * (t + 1)],
                rhs=p_words[g][:, c0:c1].bitcast(FP8X4),
                rhs_scale=p_bytes[4 * g : P, c0:c1],
                start=(g == 0),
                stop=(g == G - 1),
            )

        def layer1_b(s, t, g):
            layer1(acc_b[s][:, t, :], t, A + P * s, A + P * (s + 1), g)

        for g in range(G):
            split = (P, 64, 44)[g]
            cast_w1(g, "s", 0, split)
            if split < P:
                cast_w1(g, "v", split, P, slice(0, 2))
                cast_w1(g, "v", split, P, slice(2, 4))
            if g < 2:
                quant_w1(g, 0, 4)
            else:
                quant_w1(g, 0, 1)
                quant_w1(g, 1, 2)
                quant_w1(g, 2, 4)
            for t in range(4):
                layer1(acc_a[t][:], t, 0, A, g)
            for s in range(2):
                layer1_b(s, 0, g)
        for s in range(2):
            for t in range(1, 4):
                for g in range(G):
                    layer1_b(s, t, g)

        nc.vector.tensor_copy(
            w2_grp[:].rearrange("p (c i) j -> p c j i", i=4), w2_raw[:].rearrange("p j (c i) -> p c j i", i=4)
        )
        nc.vector.quantize_mx(
            out=w2_words[:].bitcast(FP8X4), scales=w2_bytes[:], in_=w2_grp[:].rearrange("p c j -> p (c j)")
        )

        for t in range(4):
            nc.scalar.activation(h_flat[:, t, :], acc_a[t][:], SILU)
        for s in range(2):
            nc.scalar.activation(h_grp_b[s][:], acc_b[s][:].rearrange("p t n -> p n t"), SILU)

        nc.vector.tensor_copy(
            h_grp_a[:].rearrange("p (c i) t -> p c t i", i=4), h_flat[:].rearrange("p t (c i) -> p c t i", i=4)
        )

        def quant_h(grp, c0, c1):
            nc.vector.quantize_mx(
                out=h_words[:, c0:c1].bitcast(FP8X4),
                scales=h_bytes[:, c0:c1],
                in_=grp[:].rearrange("p n t -> p (n t)"),
            )

        quant_h(h_grp_a, 0, A)
        for s in range(2):
            quant_h(h_grp_b[s], A + P * s, A + P * (s + 1))

        tags = ("acc_y0", "acc_y1", "acc_a0", "acc_a1")
        acc_y = [psum.tile([P, S], F32, name=f"acc_y{m}", tag=tags[m]) for m in range(M_TILES)]

        def layer2(m):
            for c0, c1 in ((0, A), (A, A + P), (A + P, S)):
                nc.tensor.matmul_mx(
                    out=acc_y[m][:, c0:c1],
                    lhsT=w2_words[:, P * m : P * (m + 1)].bitcast(FP8X4),
                    lhsT_scale=w2_bytes[:, P * m : P * (m + 1)],
                    rhs=h_words[:, c0:c1].bitcast(FP8X4),
                    rhs_scale=h_bytes[:, c0:c1],
                    start=True,
                    stop=True,
                )

        layer2(0)
        nc.vector.tensor_copy(y_sb[0][:, : A + P], acc_y[0][:, : A + P])
        nc.scalar.activation(y_sb[0][:, A + P :], acc_y[0][:, A + P :], COPY)
        for m in range(1, M_TILES):
            layer2(m)
            nc.scalar.activation(y_sb[m][:], acc_y[m][:], COPY)

        def fetch(m, d):
            nc.vector.tensor_tensor(terms[m][:, d, :], y_sb[m][:].indirect(pos_sb[d][:]), gates[m][:, d, :], MULT)

        def add(o, a, b):
            nc.vector.tensor_tensor(o, a, b, ADD)

        def store(m):
            nc.sync.dma_start(out=out[P * m : P * (m + 1), :], in_=sums[m][:])

        for m in range(M_TILES):
            fetch(m, 0)
            if m > 0:
                add(pairs[m - 1][:], terms[m - 1][:, 0:2, :], terms[m - 1][:, 2:4, :])
            fetch(m, 1)
            if m > 0:
                add(sums[m - 1][:], pairs[m - 1][:, 0, :], pairs[m - 1][:, 1, :])
                store(m - 1)
            fetch(m, 2)
            if m == M_TILES - 1:
                add(pairs[m][:, 0, :], terms[m][:, 0, :], terms[m][:, 1, :])
            fetch(m, 3)
        m = M_TILES - 1
        add(pairs[m][:, 1, :], pairs[m][:, 0, :], terms[m][:, 2, :])
        add(sums[m][:], pairs[m][:, 1, :], terms[m][:, 3, :])
        store(m)
